import numpy as np
import ml_dtypes


def mxq(x, axis, fmt="e4m3"):
    dtype, down = {"e4m3": (ml_dtypes.float8_e4m3fn, 7), "e5m2": (ml_dtypes.float8_e5m2, 14)}[fmt]
    v = np.moveaxis(np.asarray(x, np.float32).astype(ml_dtypes.bfloat16).astype(np.float64), axis, -1)
    blocks = v.reshape(v.shape[:-1] + (-1, 32))
    amax = np.abs(blocks).max(-1, keepdims=True)
    byte = np.maximum(np.where(amax > 0, np.frexp(amax)[1] - 1 + 127, 0) - down, 1)
    scale = np.exp2(byte - 127.0)
    codes = (blocks / scale).astype(np.float32).astype(dtype).astype(np.float64)
    return np.moveaxis((codes * scale).reshape(v.shape), -1, axis)


WIDE = False


def mx_kscale(k):
    if not WIDE:
        return np.ones(k)
    levels = np.array([10, -10, 5, -5, 0])
    if k % 512:
        return np.exp2(np.random.permutation(np.resize(levels, k // 32))).repeat(32)
    a = np.empty((k // 512, 16))
    for p in range(k // 512):
        a[p, :8] = np.random.permutation(np.resize(levels, 8))
        for g in range(8):
            far = levels[np.abs(levels - a[p, g]) >= 10]
            a[p, g + 8] = far[np.random.randint(len(far))]
    return np.exp2(a.ravel()).repeat(32)


def f64(x):
    return np.asarray(x).astype(np.float64)


def striped(idx):
    return np.tile(idx.reshape(-1, 16).T, (8, 1)).astype(np.uint16)


def unstriped(offs):
    return offs[:16].T.reshape(-1).astype(np.int64)


def relu(v):
    return np.maximum(v, 0.0)


K, T, S, V, H, N, J = 512, 2048, 1024, 512, 512, 256, 512


def setup_inputs():
    n = np.random.standard_normal
    s = mx_kscale(K)[:, None]
    u = mx_kscale(H)
    r = mx_kscale(J)[:, None]
    return {
        "xT": (n((K, T)) * s).astype(np.float32),
        "eT": (n((J, V)) * r).astype(np.float32),
        "w1": (n((K, H)) / np.sqrt(3 * K) / s * u).astype(np.float32),
        "w2": (n((K, H)) / np.sqrt(3 * K) / s * u).astype(np.float32),
        "w3": (n((J, H)) / np.sqrt(3 * J) / r * u).astype(np.float32),
        "w4": (n((H, N)) / np.sqrt(H) / u[:, None]).astype(np.float32),
        "offs": striped(np.random.permutation(T)[:S]),
    }


def reference(xT, eT, w1, w2, w3, w4, offs):
    xq = mxq(f64(xT)[:, unstriped(offs)], 0, "e4m3")
    h = relu(mxq(f64(w1), 0, "e4m3").T @ xq[:, :V] + mxq(f64(w2), 0, "e4m3").T @ xq[:, V:2 * V] + mxq(f64(w3), 0, "e4m3").T @ mxq(f64(eT), 0, "e4m3"))
    return mxq(f64(w4), 0, "e4m3").T @ mxq(h, 0, "e4m3")

@@ -1,0 +1,135 @@
+from contextlib import ExitStack
+
+import concourse.mybir as mybir
+
+K, T, S, V, H, N = 512, 2048, 1024, 512, 512, 256
+FLOPS = 2 * V * (3 * K * H + H * N)
+
+F32 = mybir.dt.float32
+BF16 = mybir.dt.bfloat16
+U32 = mybir.dt.uint32
+U16 = mybir.dt.uint16
+U8 = mybir.dt.uint8
+FP8X4 = mybir.dt.float8_e4m3fn_x4
+COPY = mybir.ActivationFunctionType.Copy
+RELU = mybir.ActivationFunctionType.Relu
+
+P = 128
+PACK = 4
+LINE = 4
+EDGES = 128
+HALF_T = T // 2
+X_VECTOR_COLS = (704, 704, 256, 704)
+W3_VECTOR_M = 96
+
+
+def cast(nc, on_vector, out, in_):
+    if on_vector:
+        nc.vector.tensor_copy(out=out, in_=in_)
+    else:
+        nc.scalar.activation(out=out, in_=in_, func=COPY)
+
+
+def quantize(nc, pool, grouped, width, name):
+    codes = pool.tile([P, width], U32, align_bytes=64, name=name + "_codes")
+    scales = pool.tile([P, width], U8, align_bytes=64, name=name + "_scales")
+    nc.vector.quantize_mx(out=codes[:].bitcast(FP8X4), scales=scales[:], in_=grouped)
+    return codes, scales
+
+
+def product(nc, out, stationary, cols, moving, edges, start, stop):
+    nc.tensor.matmul_mx(
+        out=out,
+        lhsT=stationary[0][:, cols].bitcast(FP8X4),
+        lhsT_scale=stationary[1][:, cols],
+        rhs=moving[0][:, edges].bitcast(FP8X4),
+        rhs_scale=moving[1][:, edges],
+        start=start,
+        stop=stop,
+    )
+
+
+def tile_picked_edgeup_relu_e_kernel(tc, xT, eT, w1, w2, w3, w4, offs, out):
+    nc = tc.nc
+    chunks = V // EDGES
+
+    with ExitStack() as ctx:
+        sb = ctx.enter_context(tc.tile_pool(name="sb", bufs=1))
+        psum = ctx.enter_context(tc.psum_pool(name="psum", bufs=1))
+
+        x_rows = xT.rearrange("(p j) n -> p j n", j=PACK)
+        offsets = sb.tile([P, S // 16], U16, name="offsets")
+        x_raw = {}
+        for u in range(2):
+            for h in range(2):
+                x_raw[u, h] = sb.tile([P, 2, HALF_T], F32, name="x_raw_%d%d" % (u, h))
+                nc.sync.dma_start(out=x_raw[u, h][:], in_=x_rows[:, 2 * u : 2 * u + 2, h * HALF_T : (h + 1) * HALF_T])
+                if (u, h) == (0, 0):
+                    nc.sync.dma_start(offsets[:], offs)
+        raw = {}
+        for name, src in (("w1", w1), ("w2", w2), ("w3", w3), ("e", eT), ("w4", w4)):
+            raw[name] = sb.tile([P, PACK, src.shape[1]], F32, name=name + "_raw")
+            nc.sync.dma_start(out=raw[name][:], in_=src.rearrange("(p j) n -> p j n", j=PACK))
+
+        nodes = [sb.tile([P, V * PACK], BF16, align_bytes=64, name="nodes_%d" % s) for s in range(2)]
+        for u in range(2):
+            pairs = sb.tile([P, T * 2], BF16, align_bytes=64, name="pairs_%d" % u)
+            for h in range(2):
+                split = X_VECTOR_COLS[2 * u + h]
+                for on_vector, a, b in ((True, 0, split), (False, split, HALF_T)):
+                    dst = pairs[:, 2 * (h * HALF_T + a) : 2 * (h * HALF_T + b)]
+                    cast(nc, on_vector,
+                         dst.rearrange("p (c i e) -> p c e i", i=LINE, e=2),
+                         x_raw[u, h][:, :, a:b].rearrange("p e (c i) -> p c e i", i=LINE))
+            for s in range(2):
+                words = nodes[s][:].bitcast(U32).rearrange("p (v u) -> p v u", u=2)
+                entries = offsets[:, s * V // 16 : (s + 1) * V // 16]
+                nc.vector.tensor_copy(out=words[:, :, u], in_=pairs[:].bitcast(U32).indirect(entries))
+        node_q = [quantize(nc, sb, nodes[s][:], V, "node_%d" % s) for s in range(2)]
+
+        w_q = []
+        for name, split in (("w1", 0), ("w2", 0), ("w3", W3_VECTOR_M)):
+            grouped = sb.tile([P, H * PACK], BF16, align_bytes=64, name=name + "_grouped")
+            dst = grouped[:].rearrange("p (t m j) -> p m j t", t=PACK, j=PACK)
+            src = raw[name][:].rearrange("p j (m t) -> p m j t", t=PACK)
+            if split:
+                cast(nc, True, dst[:, :split], src[:, :split])
+            cast(nc, False, dst[:, split:], src[:, split:])
+            w_q.append(quantize(nc, sb, grouped[:], H, name))
+
+        e_grouped = []
+        for c in range(chunks):
+            grouped = sb.tile([P, EDGES * PACK], BF16, align_bytes=64, name="e_grouped_%d" % c)
+            cast(nc, c != 1,
+                 grouped[:].rearrange("p (c i j) -> p c j i", i=LINE, j=PACK),
+                 raw["e"][:, :, c * EDGES : (c + 1) * EDGES].rearrange("p j (c i) -> p c j i", i=LINE))
+            e_grouped.append(grouped)
+        e_q = [quantize(nc, sb, e_grouped[c][:], EDGES, "e_%d" % c) for c in range(chunks)]
+
+        w4_grouped = sb.tile([P, N * PACK], BF16, align_bytes=64, name="w4_grouped")
+        for half in range(2):
+            cols = slice(half * P, (half + 1) * P)
+            cast(nc, half == 0,
+                 w4_grouped[:, half * P * PACK : (half + 1) * P * PACK].rearrange("p (c i j) -> p c j i", i=LINE, j=PACK),
+                 raw["w4"][:, :, cols].rearrange("p j (c i) -> p c j i", i=LINE))
+        w4_q = quantize(nc, sb, w4_grouped[:], N, "w4")
+
+        out_rows = out.rearrange("(mt p) v -> p mt v", p=P)
+        for c in range(chunks):
+            edges = slice(c * EDGES, (c + 1) * EDGES)
+            hidden = psum.tile([P, PACK, EDGES], F32, name="hidden_%d" % c)
+            for t in range(PACK):
+                cols = slice(t * P, (t + 1) * P)
+                product(nc, hidden[:, t, :], w_q[0], cols, node_q[0], edges, True, False)
+                product(nc, hidden[:, t, :], w_q[1], cols, node_q[1], edges, False, False)
+                product(nc, hidden[:, t, :], w_q[2], cols, e_q[c], slice(0, EDGES), False, True)
+            h_grouped = sb.tile([P, EDGES * PACK], BF16, align_bytes=64, name="h_grouped_%d" % c)
+            nc.scalar.activation(out=h_grouped[:].rearrange("p (v t) -> p v t", t=PACK),
+                                 in_=hidden[:].rearrange("p t v -> p v t"), func=RELU)
+            h_q = quantize(nc, sb, h_grouped[:], EDGES, "h_%d" % c)
+            result = psum.tile([P, N // P, EDGES], F32, name="result_%d" % c)
+            for mt in range(N // P):
+                product(nc, result[:, mt, :], w4_q, slice(mt * P, (mt + 1) * P), h_q, slice(0, EDGES), True, True)
+            staged = sb.tile([P, N // P, EDGES], F32, name="staged_%d" % c)
+            nc.vector.tensor_copy(out=staged[:], in_=result[:])
+            nc.sync.dma_start(out=out_rows[:, :, edges], in_=staged[:])

@@ -16,32 +16,51 @@ RELU = mybir.ActivationFunctionType.Relu
 
 P = 128
 PACK = 4
-LINE = 4
-EDGES = 128
+RUN = 4
+LIST_ROWS = 16
+MX_ALIGN = 64
 HALF_T = T // 2
-X_VECTOR_COLS = (704, 704, 256, 704)
-W3_VECTOR_M = 96
+EARLY = V // 2
+LATE = V // 4
+
+X_NODES_ON_VECTOR = ((704, 704), (0, 768))
 
 
-def cast(nc, on_vector, out, in_):
+def convert(nc, on_vector, dst, src):
     if on_vector:
-        nc.vector.tensor_copy(out=out, in_=in_)
+        nc.vector.tensor_copy(out=dst, in_=src)
     else:
-        nc.scalar.activation(out=out, in_=in_, func=COPY)
+        nc.scalar.activation(out=dst, in_=src, func=COPY)
 
 
-def quantize(nc, pool, grouped, width, name):
-    codes = pool.tile([P, width], U32, align_bytes=64, name=name + "_codes")
-    scales = pool.tile([P, width], U8, align_bytes=64, name=name + "_scales")
-    nc.vector.quantize_mx(out=codes[:].bitcast(FP8X4), scales=scales[:], in_=grouped)
+def interleave(nc, on_vector, dst, rows):
+    convert(
+        nc,
+        on_vector,
+        dst.rearrange("p (c i j) -> p c j i", i=RUN, j=rows.shape[1]),
+        rows.rearrange("p j (c i) -> p c j i", i=RUN),
+    )
+
+
+def grouped_tile(pool, columns, name):
+    return pool.tile([P, columns * PACK], BF16, align_bytes=MX_ALIGN, name=name + "_grouped")
+
+
+def quantize(nc, pool, grouped, name):
+    columns = grouped[:].shape[1] // PACK
+    codes = pool.tile([P, columns], U32, align_bytes=MX_ALIGN, name=name + "_codes")
+    scales = pool.tile([P, columns], U8, align_bytes=MX_ALIGN, name=name + "_scales")
+    nc.vector.quantize_mx(out=codes[:].bitcast(FP8X4), scales=scales[:], in_=grouped[:])
     return codes, scales
 
 
-def product(nc, out, stationary, cols, moving, edges, start, stop):
+def product(nc, acc, stationary, first_column, moving, first_edge, start, stop):
+    columns = slice(first_column, first_column + P)
+    edges = slice(first_edge, first_edge + acc.shape[1])
     nc.tensor.matmul_mx(
-        out=out,
-        lhsT=stationary[0][:, cols].bitcast(FP8X4),
-        lhsT_scale=stationary[1][:, cols],
+        out=acc,
+        lhsT=stationary[0][:, columns].bitcast(FP8X4),
+        lhsT_scale=stationary[1][:, columns],
         rhs=moving[0][:, edges].bitcast(FP8X4),
         rhs_scale=moving[1][:, edges],
         start=start,
@@ -51,85 +70,115 @@ def product(nc, out, stationary, cols, moving, edges, start, stop):
 
 def tile_picked_edgeup_relu_e_kernel(tc, xT, eT, w1, w2, w3, w4, offs, out):
     nc = tc.nc
-    chunks = V // EDGES
 
     with ExitStack() as ctx:
         sb = ctx.enter_context(tc.tile_pool(name="sb", bufs=1))
         psum = ctx.enter_context(tc.psum_pool(name="psum", bufs=1))
 
-        x_rows = xT.rearrange("(p j) n -> p j n", j=PACK)
-        offsets = sb.tile([P, S // 16], U16, name="offsets")
+        def load(name, rows):
+            tile = sb.tile(list(rows.shape), F32, name=name + "_raw")
+            nc.sync.dma_start(out=tile[:], in_=rows)
+            return tile
+
+        def by_partition(matrix):
+            return matrix.rearrange("(p j) n -> p j n", j=PACK)
+
+        offsets = sb.tile([P, S // LIST_ROWS], U16, name="offsets")
         x_raw = {}
         for u in range(2):
-            for h in range(2):
-                x_raw[u, h] = sb.tile([P, 2, HALF_T], F32, name="x_raw_%d%d" % (u, h))
-                nc.sync.dma_start(out=x_raw[u, h][:], in_=x_rows[:, 2 * u : 2 * u + 2, h * HALF_T : (h + 1) * HALF_T])
-                if (u, h) == (0, 0):
+            for half in range(2):
+                rows = by_partition(xT)[:, 2 * u : 2 * u + 2, half * HALF_T : (half + 1) * HALF_T]
+                x_raw[u, half] = load("x_%d%d" % (u, half), rows)
+                if (u, half) == (0, 0):
                     nc.sync.dma_start(offsets[:], offs)
-        raw = {}
-        for name, src in (("w1", w1), ("w2", w2), ("w3", w3), ("e", eT), ("w4", w4)):
-            raw[name] = sb.tile([P, PACK, src.shape[1]], F32, name=name + "_raw")
-            nc.sync.dma_start(out=raw[name][:], in_=src.rearrange("(p j) n -> p j n", j=PACK))
+        e_early_raw = load("e_early", by_partition(eT[:, :EARLY]))
+        w_raw = [load("w%d" % (n + 1), by_partition(w)) for n, w in enumerate((w1, w2, w3))]
+        e_late_raw = load("e_late", by_partition(eT[:, EARLY:]))
+        w4_raw = load("w4", by_partition(w4))
 
-        nodes = [sb.tile([P, V * PACK], BF16, align_bytes=64, name="nodes_%d" % s) for s in range(2)]
+        nodes = [grouped_tile(sb, V, "nodes_%d" % side) for side in range(2)]
         for u in range(2):
-            pairs = sb.tile([P, T * 2], BF16, align_bytes=64, name="pairs_%d" % u)
-            for h in range(2):
-                split = X_VECTOR_COLS[2 * u + h]
+            pairs = sb.tile([P, T * 2], BF16, align_bytes=MX_ALIGN, name="pairs_%d" % u)
+            for half in range(2):
+                split = X_NODES_ON_VECTOR[u][half]
                 for on_vector, a, b in ((True, 0, split), (False, split, HALF_T)):
-                    dst = pairs[:, 2 * (h * HALF_T + a) : 2 * (h * HALF_T + b)]
-                    cast(nc, on_vector,
-                         dst.rearrange("p (c i e) -> p c e i", i=LINE, e=2),
-                         x_raw[u, h][:, :, a:b].rearrange("p e (c i) -> p c e i", i=LINE))
-            for s in range(2):
-                words = nodes[s][:].bitcast(U32).rearrange("p (v u) -> p v u", u=2)
-                entries = offsets[:, s * V // 16 : (s + 1) * V // 16]
+                    if a < b:
+                        at = half * HALF_T
+                        interleave(nc, on_vector, pairs[:, 2 * (at + a) : 2 * (at + b)], x_raw[u, half][:, :, a:b])
+            for side in range(2):
+                words = nodes[side][:].bitcast(U32).rearrange("p (v u) -> p v u", u=2)
+                entries = offsets[:, side * V // LIST_ROWS : (side + 1) * V // LIST_ROWS]
                 nc.vector.tensor_copy(out=words[:, :, u], in_=pairs[:].bitcast(U32).indirect(entries))
-        node_q = [quantize(nc, sb, nodes[s][:], V, "node_%d" % s) for s in range(2)]
+        nodes_q = [quantize(nc, sb, nodes[side], "nodes_%d" % side) for side in range(2)]
 
         w_q = []
-        for name, split in (("w1", 0), ("w2", 0), ("w3", W3_VECTOR_M)):
-            grouped = sb.tile([P, H * PACK], BF16, align_bytes=64, name=name + "_grouped")
-            dst = grouped[:].rearrange("p (t m j) -> p m j t", t=PACK, j=PACK)
-            src = raw[name][:].rearrange("p j (m t) -> p m j t", t=PACK)
-            if split:
-                cast(nc, True, dst[:, :split], src[:, :split])
-            cast(nc, False, dst[:, split:], src[:, split:])
-            w_q.append(quantize(nc, sb, grouped[:], H, name))
+        for n in range(3):
+            channels = w_raw[n][:].rearrange("p j (m t) -> p m j t", t=PACK)
+            parts = []
+            for part in range(2):
+                grouped = grouped_tile(sb, 2 * P, "w%d_%d" % (n + 1, part))
+                dealt = grouped[:].rearrange("p (t m j) -> p m j t", t=2, j=PACK)
+                convert(nc, n > 0 and part == 0, dealt, channels[:, :, :, 2 * part : 2 * part + 2])
+                parts.append(grouped)
+            w_q.append([quantize(nc, sb, parts[part], "w%d_%d" % (n + 1, part)) for part in range(2)])
 
-        e_grouped = []
-        for c in range(chunks):
-            grouped = sb.tile([P, EDGES * PACK], BF16, align_bytes=64, name="e_grouped_%d" % c)
-            cast(nc, c != 1,
-                 grouped[:].rearrange("p (c i j) -> p c j i", i=LINE, j=PACK),
-                 raw["e"][:, :, c * EDGES : (c + 1) * EDGES].rearrange("p j (c i) -> p c j i", i=LINE))
-            e_grouped.append(grouped)
-        e_q = [quantize(nc, sb, e_grouped[c][:], EDGES, "e_%d" % c) for c in range(chunks)]
+        def hidden_sum(acc, t, first_edge, e_q):
+            part, column = t // 2, (t % 2) * P
+            product(nc, acc, w_q[0][part], column, nodes_q[0], first_edge, True, False)
+            product(nc, acc, w_q[1][part], column, nodes_q[1], first_edge, False, False)
+            product(nc, acc, w_q[2][part], column, e_q, 0, False, True)
 
-        w4_grouped = sb.tile([P, N * PACK], BF16, align_bytes=64, name="w4_grouped")
-        for half in range(2):
-            cols = slice(half * P, (half + 1) * P)
-            cast(nc, half == 0,
-                 w4_grouped[:, half * P * PACK : (half + 1) * P * PACK].rearrange("p (c i j) -> p c j i", i=LINE, j=PACK),
-                 raw["w4"][:, :, cols].rearrange("p j (c i) -> p c j i", i=LINE))
-        w4_q = quantize(nc, sb, w4_grouped[:], N, "w4")
+        e_early = grouped_tile(sb, EARLY, "e_early")
+        interleave(nc, False, e_early[:], e_early_raw[:])
+        e_early_q = quantize(nc, sb, e_early, "e_early")
+        early_banks = []
+        for t in range(PACK):
+            bank = psum.tile([P, EARLY], F32, name="early_bank_%d" % t, tag="early_bank_%d" % t)
+            hidden_sum(bank[:], t, 0, e_early_q)
+            early_banks.append(bank)
 
-        out_rows = out.rearrange("(mt p) v -> p mt v", p=P)
-        for c in range(chunks):
-            edges = slice(c * EDGES, (c + 1) * EDGES)
-            hidden = psum.tile([P, PACK, EDGES], F32, name="hidden_%d" % c)
+        late_banks = []
+        for g in range(2):
+            e_late = grouped_tile(sb, LATE, "e_late_%d" % g)
+            interleave(nc, g == 0, e_late[:], e_late_raw[:, :, g * LATE : (g + 1) * LATE])
+            e_late_q = quantize(nc, sb, e_late, "e_late_%d" % g)
+            bank = psum.tile([P, PACK, LATE], F32, name="late_bank_%d" % g)
             for t in range(PACK):
-                cols = slice(t * P, (t + 1) * P)
-                product(nc, hidden[:, t, :], w_q[0], cols, node_q[0], edges, True, False)
-                product(nc, hidden[:, t, :], w_q[1], cols, node_q[1], edges, False, False)
-                product(nc, hidden[:, t, :], w_q[2], cols, e_q[c], slice(0, EDGES), False, True)
-            h_grouped = sb.tile([P, EDGES * PACK], BF16, align_bytes=64, name="h_grouped_%d" % c)
-            nc.scalar.activation(out=h_grouped[:].rearrange("p (v t) -> p v t", t=PACK),
-                                 in_=hidden[:].rearrange("p t v -> p v t"), func=RELU)
-            h_q = quantize(nc, sb, h_grouped[:], EDGES, "h_%d" % c)
-            result = psum.tile([P, N // P, EDGES], F32, name="result_%d" % c)
-            for mt in range(N // P):
-                product(nc, result[:, mt, :], w4_q, slice(mt * P, (mt + 1) * P), h_q, slice(0, EDGES), True, True)
-            staged = sb.tile([P, N // P, EDGES], F32, name="staged_%d" % c)
-            nc.vector.tensor_copy(out=staged[:], in_=result[:])
-            nc.sync.dma_start(out=out_rows[:, :, edges], in_=staged[:])
+                hidden_sum(bank[:, t, :], t, EARLY + g * LATE, e_late_q)
+            late_banks.append(bank)
+
+        w4_grouped = grouped_tile(sb, N, "w4")
+        interleave(nc, True, w4_grouped[:], w4_raw[:])
+        w4_q = quantize(nc, sb, w4_grouped, "w4")
+
+        out_rows = out.rearrange("(r p) v -> p r v", p=P)
+        row_tiles = N // P
+
+        h_tiles = sb.tile([P, PACK, EARLY], BF16, align_bytes=MX_ALIGN, name="h_tiles")
+        for t in range(PACK):
+            nc.scalar.activation(out=h_tiles[:, t, :], in_=early_banks[t][:], func=RELU)
+        h_early = grouped_tile(sb, EARLY, "h_early")
+        interleave(nc, True, h_early[:], h_tiles[:])
+        h_early_q = quantize(nc, sb, h_early, "h_early")
+        for r in range(row_tiles):
+            result = psum.tile([P, EARLY], F32, name="early_result_%d" % r, tag="early_bank_%d" % r)
+            product(nc, result[:], w4_q, r * P, h_early_q, 0, True, True)
+            staged = sb.tile([P, EARLY], F32, name="early_staged_%d" % r)
+            convert(nc, r == 0, staged[:], result[:])
+            nc.sync.dma_start(out=out_rows[:, r, :EARLY], in_=staged[:])
+
+        for g in range(2):
+            h_late = grouped_tile(sb, LATE, "h_late_%d" % g)
+            nc.scalar.activation(
+                out=h_late[:].rearrange("p (v t) -> p v t", t=PACK),
+                in_=late_banks[g][:].rearrange("p t v -> p v t"),
+                func=RELU,
+            )
+            h_late_q = quantize(nc, sb, h_late, "h_late_%d" % g)
+            result = psum.tile([P, row_tiles, LATE], F32, name="late_result_%d" % g)
+            for r in range(row_tiles):
+                product(nc, result[:, r, :], w4_q, r * P, h_late_q, 0, True, True)
+            staged = sb.tile([P, row_tiles, LATE], F32, name="late_staged_%d" % g)
+            convert(nc, g == 1, staged[:], result[:])
+            first_edge = EARLY + g * LATE
+            nc.sync.dma_start(out=out_rows[:, :, first_edge : first_edge + LATE], in_=staged[:])

from contextlib import ExitStack

import concourse.mybir as mybir

K, T, S, V, H, N = 512, 2048, 1024, 512, 512, 256
FLOPS = 2 * V * (3 * K * H + H * N)

F32 = mybir.dt.float32
BF16 = mybir.dt.bfloat16
U32 = mybir.dt.uint32
U16 = mybir.dt.uint16
U8 = mybir.dt.uint8
FP8X4 = mybir.dt.float8_e4m3fn_x4
COPY = mybir.ActivationFunctionType.Copy
RELU = mybir.ActivationFunctionType.Relu

P = 128
PACK = 4
RUN = 4
LIST_ROWS = 16
MX_ALIGN = 64
HALF_T = T // 2
EARLY = V // 2
LATE = V // 4

X_NODES_ON_VECTOR = ((704, 704), (0, 768))


def convert(nc, on_vector, dst, src):
    if on_vector:
        nc.vector.tensor_copy(out=dst, in_=src)
    else:
        nc.scalar.activation(out=dst, in_=src, func=COPY)


def interleave(nc, on_vector, dst, rows):
    convert(
        nc,
        on_vector,
        dst.rearrange("p (c i j) -> p c j i", i=RUN, j=rows.shape[1]),
        rows.rearrange("p j (c i) -> p c j i", i=RUN),
    )


def grouped_tile(pool, columns, name):
    return pool.tile([P, columns * PACK], BF16, align_bytes=MX_ALIGN, name=name + "_grouped")


def quantize(nc, pool, grouped, name):
    columns = grouped[:].shape[1] // PACK
    codes = pool.tile([P, columns], U32, align_bytes=MX_ALIGN, name=name + "_codes")
    scales = pool.tile([P, columns], U8, align_bytes=MX_ALIGN, name=name + "_scales")
    nc.vector.quantize_mx(out=codes[:].bitcast(FP8X4), scales=scales[:], in_=grouped[:])
    return codes, scales


def product(nc, acc, stationary, first_column, moving, first_edge, start, stop):
    columns = slice(first_column, first_column + P)
    edges = slice(first_edge, first_edge + acc.shape[1])
    nc.tensor.matmul_mx(
        out=acc,
        lhsT=stationary[0][:, columns].bitcast(FP8X4),
        lhsT_scale=stationary[1][:, columns],
        rhs=moving[0][:, edges].bitcast(FP8X4),
        rhs_scale=moving[1][:, edges],
        start=start,
        stop=stop,
    )


def tile_picked_edgeup_relu_e_kernel(tc, xT, eT, w1, w2, w3, w4, offs, out):
    nc = tc.nc

    with ExitStack() as ctx:
        sb = ctx.enter_context(tc.tile_pool(name="sb", bufs=1))
        psum = ctx.enter_context(tc.psum_pool(name="psum", bufs=1))

        def load(name, rows):
            tile = sb.tile(list(rows.shape), F32, name=name + "_raw")
            nc.sync.dma_start(out=tile[:], in_=rows)
            return tile

        def by_partition(matrix):
            return matrix.rearrange("(p j) n -> p j n", j=PACK)

        offsets = sb.tile([P, S // LIST_ROWS], U16, name="offsets")
        x_raw = {}
        for u in range(2):
            for half in range(2):
                rows = by_partition(xT)[:, 2 * u : 2 * u + 2, half * HALF_T : (half + 1) * HALF_T]
                x_raw[u, half] = load("x_%d%d" % (u, half), rows)
                if (u, half) == (0, 0):
                    nc.sync.dma_start(offsets[:], offs)
        e_early_raw = load("e_early", by_partition(eT[:, :EARLY]))
        w_raw = [load("w%d" % (n + 1), by_partition(w)) for n, w in enumerate((w1, w2, w3))]
        e_late_raw = load("e_late", by_partition(eT[:, EARLY:]))
        w4_raw = load("w4", by_partition(w4))

        nodes = [grouped_tile(sb, V, "nodes_%d" % side) for side in range(2)]
        for u in range(2):
            pairs = sb.tile([P, T * 2], BF16, align_bytes=MX_ALIGN, name="pairs_%d" % u)
            for half in range(2):
                split = X_NODES_ON_VECTOR[u][half]
                for on_vector, a, b in ((True, 0, split), (False, split, HALF_T)):
                    if a < b:
                        at = half * HALF_T
                        interleave(nc, on_vector, pairs[:, 2 * (at + a) : 2 * (at + b)], x_raw[u, half][:, :, a:b])
            for side in range(2):
                words = nodes[side][:].bitcast(U32).rearrange("p (v u) -> p v u", u=2)
                entries = offsets[:, side * V // LIST_ROWS : (side + 1) * V // LIST_ROWS]
                nc.vector.tensor_copy(out=words[:, :, u], in_=pairs[:].bitcast(U32).indirect(entries))
        nodes_q = [quantize(nc, sb, nodes[side], "nodes_%d" % side) for side in range(2)]

        w_q = []
        for n in range(3):
            channels = w_raw[n][:].rearrange("p j (m t) -> p m j t", t=PACK)
            parts = []
            for part in range(2):
                grouped = grouped_tile(sb, 2 * P, "w%d_%d" % (n + 1, part))
                dealt = grouped[:].rearrange("p (t m j) -> p m j t", t=2, j=PACK)
                convert(nc, n > 0 and part == 0, dealt, channels[:, :, :, 2 * part : 2 * part + 2])
                parts.append(grouped)
            w_q.append([quantize(nc, sb, parts[part], "w%d_%d" % (n + 1, part)) for part in range(2)])

        def hidden_sum(acc, t, first_edge, e_q):
            part, column = t // 2, (t % 2) * P
            product(nc, acc, w_q[0][part], column, nodes_q[0], first_edge, True, False)
            product(nc, acc, w_q[1][part], column, nodes_q[1], first_edge, False, False)
            product(nc, acc, w_q[2][part], column, e_q, 0, False, True)

        e_early = grouped_tile(sb, EARLY, "e_early")
        interleave(nc, False, e_early[:], e_early_raw[:])
        e_early_q = quantize(nc, sb, e_early, "e_early")
        early_banks = []
        for t in range(PACK):
            bank = psum.tile([P, EARLY], F32, name="early_bank_%d" % t, tag="early_bank_%d" % t)
            hidden_sum(bank[:], t, 0, e_early_q)
            early_banks.append(bank)

        late_banks = []
        for g in range(2):
            e_late = grouped_tile(sb, LATE, "e_late_%d" % g)
            interleave(nc, g == 0, e_late[:], e_late_raw[:, :, g * LATE : (g + 1) * LATE])
            e_late_q = quantize(nc, sb, e_late, "e_late_%d" % g)
            bank = psum.tile([P, PACK, LATE], F32, name="late_bank_%d" % g)
            for t in range(PACK):
                hidden_sum(bank[:, t, :], t, EARLY + g * LATE, e_late_q)
            late_banks.append(bank)

        w4_grouped = grouped_tile(sb, N, "w4")
        interleave(nc, True, w4_grouped[:], w4_raw[:])
        w4_q = quantize(nc, sb, w4_grouped, "w4")

        out_rows = out.rearrange("(r p) v -> p r v", p=P)
        row_tiles = N // P

        h_tiles = sb.tile([P, PACK, EARLY], BF16, align_bytes=MX_ALIGN, name="h_tiles")
        for t in range(PACK):
            nc.scalar.activation(out=h_tiles[:, t, :], in_=early_banks[t][:], func=RELU)
        h_early = grouped_tile(sb, EARLY, "h_early")
        interleave(nc, True, h_early[:], h_tiles[:])
        h_early_q = quantize(nc, sb, h_early, "h_early")
        for r in range(row_tiles):
            result = psum.tile([P, EARLY], F32, name="early_result_%d" % r, tag="early_bank_%d" % r)
            product(nc, result[:], w4_q, r * P, h_early_q, 0, True, True)
            staged = sb.tile([P, EARLY], F32, name="early_staged_%d" % r)
            convert(nc, r == 0, staged[:], result[:])
            nc.sync.dma_start(out=out_rows[:, r, :EARLY], in_=staged[:])

        for g in range(2):
            h_late = grouped_tile(sb, LATE, "h_late_%d" % g)
            nc.scalar.activation(
                out=h_late[:].rearrange("p (v t) -> p v t", t=PACK),
                in_=late_banks[g][:].rearrange("p t v -> p v t"),
                func=RELU,
            )
            h_late_q = quantize(nc, sb, h_late, "h_late_%d" % g)
            result = psum.tile([P, row_tiles, LATE], F32, name="late_result_%d" % g)
            for r in range(row_tiles):
                product(nc, result[:, r, :], w4_q, r * P, h_late_q, 0, True, True)
            staged = sb.tile([P, row_tiles, LATE], F32, name="late_staged_%d" % g)
            convert(nc, g == 1, staged[:], result[:])
            first_edge = EARLY + g * LATE
            nc.sync.dma_start(out=out_rows[:, :, first_edge : first_edge + LATE], in_=staged[:])
